import numpy as np
import ml_dtypes


def mxq(x, axis, fmt="e4m3"):
    dtype, down = {"e4m3": (ml_dtypes.float8_e4m3fn, 7), "e5m2": (ml_dtypes.float8_e5m2, 14)}[fmt]
    v = np.moveaxis(np.asarray(x, np.float32).astype(ml_dtypes.bfloat16).astype(np.float64), axis, -1)
    blocks = v.reshape(v.shape[:-1] + (-1, 32))
    amax = np.abs(blocks).max(-1, keepdims=True)
    byte = np.maximum(np.where(amax > 0, np.frexp(amax)[1] - 1 + 127, 0) - down, 1)
    scale = np.exp2(byte - 127.0)
    codes = (blocks / scale).astype(np.float32).astype(dtype).astype(np.float64)
    return np.moveaxis((codes * scale).reshape(v.shape), -1, axis)


WIDE = False


def mx_kscale(k):
    if not WIDE:
        return np.ones(k)
    levels = np.array([10, -10, 5, -5, 0])
    if k % 512:
        return np.exp2(np.random.permutation(np.resize(levels, k // 32))).repeat(32)
    a = np.empty((k // 512, 16))
    for p in range(k // 512):
        a[p, :8] = np.random.permutation(np.resize(levels, 8))
        for g in range(8):
            far = levels[np.abs(levels - a[p, g]) >= 10]
            a[p, g + 8] = far[np.random.randint(len(far))]
    return np.exp2(a.ravel()).repeat(32)


BF16 = ml_dtypes.bfloat16


def bf(x):
    return np.asarray(x, np.float32).astype(BF16)


def f64(x):
    return np.asarray(x).astype(np.float64)


E2M1 = np.array([0.0, 0.5, 1.0, 1.5, 2.0, 3.0, 4.0, 6.0, -0.0, -0.5, -1.0, -1.5, -2.0, -3.0, -4.0, -6.0])


def pack_weight(w, fmt):
    k, n = w.shape
    w = f64(bf(w)).reshape(k // 32, 32, n)
    amax = np.abs(w).max(1)
    if fmt == "e4m3":
        byte = np.frexp(amax)[1] - 1 + 127 - 7
    else:
        mant, ex = np.frexp(amax / 6.0)
        byte = np.where(mant > 0.5, ex, ex - 1) + 127
    byte = np.clip(np.where(amax > 0, byte, 1), 1, 254)
    scaled = (w * np.exp2(127.0 - byte)[:, None, :]).reshape(k, n).astype(np.float32)
    by_word = np.ascontiguousarray(scaled.reshape(k // 512, 128, 4, n).transpose(0, 1, 3, 2))
    if fmt == "e4m3":
        words = by_word.astype(ml_dtypes.float8_e4m3fn).view(np.uint8)
    else:
        c = by_word.astype(ml_dtypes.float4_e2m1fn).view(np.uint8) & 0xF
        words = c[..., 0::2] | (c[..., 1::2] << 4)
    return np.ascontiguousarray(words), np.ascontiguousarray(byte.astype(np.uint8).reshape(k // 512, 16, n))


def unpack_weight(words, scales, fmt):
    g, p, n, _ = words.shape
    if fmt == "e4m3":
        vals = np.ascontiguousarray(words).view(ml_dtypes.float8_e4m3fn).astype(np.float64)
    else:
        nib = np.empty((g, p, n, 4), np.uint8)
        nib[..., 0::2] = words & 0xF
        nib[..., 1::2] = words >> 4
        vals = E2M1[nib]
    vals = vals * np.repeat(np.exp2(scales.astype(np.float64) - 127.0), 8, axis=1)[..., None]
    return vals.transpose(0, 1, 3, 2).reshape(g * 512, n)
def pack4(w):
    words, scales = pack_weight(w, "e2m1")
    return words.reshape(words.shape[0], 128, -1), scales


def unpack4(words, scales):
    return unpack_weight(words.reshape(words.shape[0], 128, -1, 2), scales, "e2m1")


G, P, J, I, R = 6, 512, 512, 1024, 512

MILES_TO_MINUTES = 36.0
TARGET = 8.0
SPREAD = 1.5


def setup_inputs():
    s = mx_kscale(G * J).reshape(G, J)
    t = mx_kscale(G * I).reshape(G, I)
    load = -np.exp(1.5 * np.random.standard_normal((G, P, J))) * 3.0 / J
    station = np.random.uniform(0.0, 1.0, (J, 1, 2))
    zone = np.random.uniform(0.0, 1.0, (1, I, 2))
    dist = np.sqrt(((station - zone) ** 2).sum(-1))
    slow = np.exp(0.15 * np.random.standard_normal((G, 1, 1)) + 0.2 * np.random.standard_normal((G, J, I)))
    kern = 1.0 / (1.0 + np.exp((MILES_TO_MINUTES * dist * slow - TARGET) / SPREAD))
    demand = np.exp(0.5 * np.random.standard_normal((G, I)))
    readout = np.random.standard_normal((G, I, R)) / np.sqrt(I)
    kern_words, kern_scales = pack4((kern / s[:, :, None]).reshape(G * J, I))
    read_words, read_scales = pack4((readout / t[:, :, None]).reshape(G * I, R))
    return {"load": bf(load * s[:, None, :]),
            "kern_words": kern_words, "kern_scales": kern_scales,
            "demand": bf(demand * t),
            "read_words": read_words, "read_scales": read_scales}


def reference(load, kern_words, kern_scales, demand, read_words, read_scales):
    kern = unpack4(kern_words, kern_scales).reshape(G, J, I)
    readout = unpack4(read_words, read_scales).reshape(G, I, R)
    logbusy = mxq(f64(load), 2, "e4m3") @ kern
    covered = (1.0 - np.exp(logbusy)) * f64(demand)[:, None, :]
    return mxq(covered, 2, "e4m3") @ readout

@@ -1,0 +1,257 @@
+from contextlib import ExitStack
+
+import concourse.mybir as mybir
+from concourse.masks import make_identity
+
+G, PLANS, J, I, R = 6, 512, 512, 1024, 512
+FLOPS = 2 * G * PLANS * (J * I + I * R)
+
+F32 = mybir.dt.float32
+BF16 = mybir.dt.bfloat16
+I32 = mybir.dt.int32
+U32 = mybir.dt.uint32
+U8 = mybir.dt.uint8
+FP8X4 = mybir.dt.float8_e4m3fn_x4
+FP4X4 = mybir.dt.float4_e2m1fn_x4
+ALU = mybir.AluOpType
+ACT = mybir.ActivationFunctionType
+
+P = 128
+PACK = 4
+TILES = PLANS // P
+PASSES = I // 512
+STEPS = G * TILES
+
+
+def tile_ambulance_expected_coverage_s14_kernel(
+    tc, load, kern_words, kern_scales, demand, read_words, read_scales, out
+):
+    nc = tc.nc
+    with ExitStack() as ctx:
+        keep = ctx.enter_context(tc.tile_pool(name="keep", bufs=1))
+        work = ctx.enter_context(tc.tile_pool(name="work", bufs=3))
+        psum = ctx.enter_context(tc.psum_pool(name="psum", bufs=2))
+        ctx.enter_context(tc.manual_schedule())
+
+        x_raw, k_raw, r_words = {}, {}, {}
+        x_bank, x_group, x_codes, x_scales = {}, {}, {}, {}
+        k_words, k_scales = {}, {}
+        busy, covered, c_codes, c_scales, acc2 = {}, {}, {}, {}, {}
+
+        def load_x(c, k):
+            t = keep.tile([P, 2, J], BF16, name="x_raw_%d_%d" % (c, k))
+            nc.sync.dma_start(out=t[:], in_=load[c].rearrange("(p b) j -> p b j", b=TILES)[:, 2 * k : 2 * k + 2, :])
+            x_raw[2 * c + k] = t
+
+        def load_kern(c):
+            t = keep.tile([P, 2 * I], U8, name="k_raw_%d" % c, align_bytes=64)
+            nc.sync.dma_start(out=t[:].bitcast(I32), in_=kern_words[c].bitcast(I32))
+            k_raw[c] = t
+
+        def load_read(c):
+            t = keep.tile([P, PASSES, 2 * R], U8, name="r_words_%d" % c, align_bytes=64)
+            nc.sync.dma_start(
+                out=t[:].bitcast(I32),
+                in_=read_words[PASSES * c : PASSES * (c + 1)].rearrange("h p n -> p h n").bitcast(I32),
+            )
+            r_words[c] = t
+
+        def load_scale_rows(plane, rows):
+            for q in range(4):
+                nc.sync.dma_start(
+                    out=plane[32 * q : 32 * q + 4].bitcast(I32),
+                    in_=rows[:, 4 * q : 4 * q + 4, :].rearrange("g r n -> r g n").bitcast(I32),
+                )
+
+        ks_first = keep.tile([P, 1, I], U8, name="ks_first", align_bytes=64)
+        ks_rest = keep.tile([P, G - 1, I], U8, name="ks_rest", align_bytes=64)
+        r_scales = keep.tile([P, G * PASSES, R], U8, name="r_scales", align_bytes=64)
+        d_rows = keep.tile([G * PASSES, 512], BF16, name="d_rows")
+        d_neg = keep.tile([P, 512], F32, name="d_neg")
+        ident = keep.tile([P, P], F32, name="ident")
+        warm = keep.tile([P, 1], F32, name="warm")
+
+        nc.scalar.dma_start(out=d_rows[:], in_=demand.rearrange("c (h i) -> (c h) i", h=PASSES))
+        nc.vector.memset(ks_first[:].bitcast(I32), 0)
+        nc.vector.memset(warm[:], 0.0)
+        nc.vector.memset(d_neg[:], 0.0)
+        nc.vector.memset(ks_rest[:].bitcast(I32), 0)
+        make_identity(nc, ident[:])
+        nc.gpsimd.memset(r_scales[:].bitcast(I32), 0)
+        nc.scalar.activation(out=warm[:], in_=warm[:], func=ACT.Exp)
+
+        load_x(0, 0)
+        load_kern(0)
+        load_scale_rows(ks_first, kern_scales[0:1])
+        load_x(0, 1)
+        load_kern(1)
+        load_x(1, 0)
+        load_scale_rows(r_scales, read_scales)
+        load_read(0)
+        load_scale_rows(ks_rest, kern_scales[1:G])
+        load_x(1, 1)
+        load_kern(2)
+        load_x(2, 0)
+        load_read(1)
+        load_x(2, 1)
+
+        def transpose_x(half):
+            bank = psum.tile([P, 2, 2, P], F32, name="x_bank", tag="x_bank", bufs=2)
+            for b in range(2):
+                words = x_raw[half][:, b, :].bitcast(F32)
+                for u in range(2):
+                    nc.tensor.transpose(bank[:, b, u, :], words[:, u : J // 2 : 2], ident[:])
+            x_bank[half] = bank
+
+        def copy_x(half):
+            t = work.tile([P, 2, P, 2], F32, name="x_group", tag="x_group", bufs=2, align_bytes=64)
+            nc.scalar.copy(out=t[:], in_=x_bank[half][:].rearrange("p b u n -> p b n u"))
+            x_group[half] = t
+
+        def quantize_x(half):
+            codes = work.tile([P, 2 * P], U32, name="x_codes", tag="x_codes", bufs=3, align_bytes=64)
+            scales = work.tile([P, 2 * P], U8, name="x_scales", tag="x_scales", bufs=3, align_bytes=64)
+            nc.vector.quantize_mx(
+                out=codes[:].bitcast(FP8X4),
+                scales=scales[:],
+                in_=x_group[half][:].rearrange("p b n u -> p (b n u)").bitcast(BF16),
+            )
+            x_codes[half], x_scales[half] = codes, scales
+
+        def sort_kern_words(c, h):
+            t = keep.tile([P, PACK, 2 * P], U8, name="k_words_%d_%d" % (c, h), align_bytes=64)
+            nc.vector.tensor_copy(
+                out=t[:].rearrange("p t (a m y) -> p a t m y", m=8, y=2),
+                in_=k_raw[c][:, 1024 * h : 1024 * (h + 1)].rearrange("p (a m t y) -> p a t m y", m=8, t=PACK, y=2),
+            )
+            k_words[c, h] = t
+
+        def sort_kern_scales(c, h):
+            raw = ks_first[:, 0, :] if c == 0 else ks_rest[:, c - 1, :]
+            t = keep.tile([P, PACK, P], U8, name="k_scales_%d_%d" % (c, h), align_bytes=64)
+            nc.vector.tensor_copy(
+                out=t[:], in_=raw[:, 512 * h : 512 * (h + 1)].rearrange("p (m t) -> p t m", t=PACK)
+            )
+            k_scales[c, h] = t
+
+        def first_matmul(s, h):
+            c, b = divmod(s, TILES)
+            half, cols = s // 2, slice((s % 2) * P, (s % 2 + 1) * P)
+            bank = psum.tile([P, PACK, P], F32, name="acc1", tag="acc1", bufs=3)
+            for t in range(PACK):
+                nc.tensor.matmul_mx(
+                    out=bank[:, t, :],
+                    lhsT=k_words[c, h][:, t, :].bitcast(FP4X4),
+                    lhsT_scale=k_scales[c, h][:, t, :],
+                    rhs=x_codes[half][:, cols].bitcast(FP8X4),
+                    rhs_scale=x_scales[half][:, cols],
+                    start=True,
+                    stop=True,
+                )
+            return bank
+
+        def exponential(s, h, bank):
+            t = work.tile([P, P, PACK], F32, name="busy", tag="busy", bufs=6)
+            nc.scalar.activation(out=t[:], in_=bank[:].rearrange("p t n -> p n t"), func=ACT.Exp)
+            busy[s, h] = t
+
+        def cover(s, h):
+            if h == 0:
+                covered[s] = work.tile([P, PASSES, P, PACK], BF16, name="covered", tag="covered", bufs=3, align_bytes=64)
+            row = PASSES * (s // TILES) + h
+            nc.vector.scalar_tensor_tensor(
+                out=covered[s][:, h],
+                in0=busy[s, h][:],
+                scalar=1.0,
+                in1=d_bank[:, row : row + 1, :].to_broadcast([P, P, PACK]),
+                op0=ALU.subtract,
+                op1=ALU.mult,
+            )
+
+        def quantize_covered(s):
+            codes = work.tile([P, PASSES * P], U32, name="c_codes", tag="c_codes", bufs=3, align_bytes=64)
+            scales = work.tile([P, PASSES * P], U8, name="c_scales", tag="c_scales", bufs=3, align_bytes=64)
+            nc.vector.quantize_mx(
+                out=codes[:].bitcast(FP8X4),
+                scales=scales[:],
+                in_=covered[s][:].rearrange("p h n t -> p (h n t)"),
+            )
+            c_codes[s], c_scales[s] = codes, scales
+
+        def second_matmul(s):
+            c = s // TILES
+            bank = psum.tile([P, R], F32, name="acc2", tag="acc2", bufs=2)
+            for h in range(PASSES):
+                nc.tensor.matmul_mx(
+                    out=bank[:],
+                    lhsT=c_codes[s][:, h * P : (h + 1) * P].bitcast(FP8X4),
+                    lhsT_scale=c_scales[s][:, h * P : (h + 1) * P],
+                    rhs=r_words[c][:, h, :].bitcast(FP4X4),
+                    rhs_scale=r_scales[:, PASSES * c + h, :],
+                    start=(h == 0),
+                    stop=(h == PASSES - 1),
+                )
+            acc2[s] = bank
+
+        def store(s):
+            c, b = divmod(s, TILES)
+            t = work.tile([P, R], F32, name="result", tag="result", bufs=4)
+            nc.scalar.copy(out=t[:], in_=acc2[s][:])
+            nc.sync.dma_start(out=out[c].rearrange("(p b) r -> p b r", b=TILES)[:, b, :], in_=t[:])
+
+        transpose_x(0)
+        copy_x(0)
+        sort_kern_words(0, 0)
+        sort_kern_scales(0, 0)
+        quantize_x(0)
+        nc.vector.tensor_scalar(
+            out=d_neg[0 : G * PASSES, :], in0=d_rows[:], scalar1=-1.0, scalar2=None, op0=ALU.mult
+        )
+        d_bank = psum.tile([P, P, PACK], F32, name="d_bank", tag="d_bank", bufs=1)
+        sort_kern_words(0, 1)
+        sort_kern_scales(0, 1)
+        transpose_x(1)
+        copy_x(1)
+        sort_kern_words(1, 0)
+
+        for s in range(STEPS + 3):
+            c, b = divmod(s, TILES)
+            if s < STEPS:
+                bank0 = first_matmul(s, 0)
+            if s >= 3:
+                second_matmul(s - 3)
+                store(s - 3)
+            if s < STEPS:
+                exponential(s, 0, bank0)
+                bank1 = first_matmul(s, 1)
+                if s == 0:
+                    for t in range(PACK):
+                        nc.tensor.transpose(d_bank[:, :, t], d_neg[:, t:512:PACK], ident[:])
+                if s % 2 == 1 and (s + 3) // 2 < 2 * G:
+                    copy_x((s + 3) // 2)
+                exponential(s, 1, bank1)
+                if s % 2 == 0 and (s + 4) // 2 < 2 * G:
+                    transpose_x((s + 4) // 2)
+            if 1 <= s <= STEPS:
+                cover(s - 1, 0)
+            if 2 <= s <= STEPS + 1:
+                quantize_covered(s - 2)
+            if 1 <= s <= STEPS:
+                cover(s - 1, 1)
+            if s % 2 == 0 and (s + 2) // 2 < 2 * G:
+                quantize_x((s + 2) // 2)
+            if b % 2 == 0 and c + 1 < G:
+                sort_kern_scales(c + 1, b // 2)
+            if b == 1 and c + 1 < G:
+                sort_kern_words(c + 1, 1)
+            if b == 3 and c + 2 < G:
+                sort_kern_words(c + 2, 0)
+            if c + 3 < G:
+                if b == 0:
+                    load_kern(c + 3)
+                if b == 1:
+                    load_x(c + 3, 0)
+                if b == 3:
+                    load_x(c + 3, 1)
+            if b == 2 and c + 2 < G:
+                load_read(c + 2)

@@ -20,7 +20,8 @@ P = 128
 PACK = 4
 TILES = PLANS // P
 PASSES = I // 512
-STEPS = G * TILES
+STEPS = 2 * G
+STACK = 4
 
 
 def tile_ambulance_expected_coverage_s14_kernel(
@@ -35,13 +36,14 @@ def tile_ambulance_expected_coverage_s14_kernel(
 
         x_raw, k_raw, r_words = {}, {}, {}
         x_bank, x_group, x_codes, x_scales = {}, {}, {}, {}
-        k_words, k_scales = {}, {}
-        busy, covered, c_codes, c_scales, acc2 = {}, {}, {}, {}, {}
+        k_words, k_scales, k_sorted = {}, {}, {}
+        acc1, busy, covered, c_codes, c_scales, acc2, result = {}, {}, {}, {}, {}, {}, {}
 
-        def load_x(c, k):
-            t = keep.tile([P, 2, J], BF16, name="x_raw_%d_%d" % (c, k))
+        def load_x(s):
+            c, k = divmod(s, 2)
+            t = keep.tile([P, 2, J], BF16, name="x_raw_%d" % s)
             nc.sync.dma_start(out=t[:], in_=load[c].rearrange("(p b) j -> p b j", b=TILES)[:, 2 * k : 2 * k + 2, :])
-            x_raw[2 * c + k] = t
+            x_raw[s] = t
 
         def load_kern(c):
             t = keep.tile([P, 2 * I], U8, name="k_raw_%d" % c, align_bytes=64)
@@ -56,202 +58,296 @@ def tile_ambulance_expected_coverage_s14_kernel(
             )
             r_words[c] = t
 
-        def load_scale_rows(plane, rows):
+        def load_read_scales(c):
+            rows = slice(PASSES * c, PASSES * (c + 2))
             for q in range(4):
                 nc.sync.dma_start(
-                    out=plane[32 * q : 32 * q + 4].bitcast(I32),
-                    in_=rows[:, 4 * q : 4 * q + 4, :].rearrange("g r n -> r g n").bitcast(I32),
+                    out=r_scales[32 * q : 32 * q + 4, rows, :].bitcast(I32),
+                    in_=read_scales[rows, 4 * q : 4 * q + 4, :].rearrange("g r n -> r g n").bitcast(I32),
                 )
 
-        ks_first = keep.tile([P, 1, I], U8, name="ks_first", align_bytes=64)
-        ks_rest = keep.tile([P, G - 1, I], U8, name="ks_rest", align_bytes=64)
+        def load_kern_scales(stack):
+            first = STACK * stack
+            n = min(STACK, G - first)
+            for q in range(4):
+                nc.sync.dma_start(
+                    out=ks_raw[stack][32 * q : 32 * q + 4 * n, :].bitcast(I32),
+                    in_=kern_scales[first : first + n, 4 * q : 4 * q + 4, :].bitcast(I32),
+                )
+
+        def sort_kern_scales(stack):
+            t = keep.tile([P, I], U8, name="ks_sorted_%d" % stack, align_bytes=64)
+            nc.vector.tensor_copy(
+                out=t[:].rearrange("p (h t m) -> p h t m", h=PASSES, t=PACK),
+                in_=ks_raw[stack][:].rearrange("p (h m t) -> p h t m", h=PASSES, t=PACK),
+            )
+            k_sorted[stack] = t
+            k_scales[STACK * stack] = t
+
+        def shift_kern_scales(c):
+            stack, level = divmod(c, STACK)
+            for q in range(4):
+                nc.sync.dma_start(
+                    out=k_scales[c][32 * q : 32 * q + 4, :].bitcast(I32),
+                    in_=k_sorted[stack][32 * q + 4 * level : 32 * q + 4 * level + 4, :].bitcast(I32),
+                )
+
+        ks_raw = [keep.tile([P, I], U8, name="ks_raw_%d" % n, align_bytes=64) for n in range(2)]
+        for c in range(G):
+            if c % STACK:
+                k_scales[c] = keep.tile([P, I], U8, name="k_scales_%d" % c, align_bytes=64)
         r_scales = keep.tile([P, G * PASSES, R], U8, name="r_scales", align_bytes=64)
-        d_rows = keep.tile([G * PASSES, 512], BF16, name="d_rows")
-        d_neg = keep.tile([P, 512], F32, name="d_neg")
+        d_raw = keep.tile([P, G * PASSES, PACK], BF16, name="d_raw")
+        d_neg = keep.tile([P, G * PASSES, PACK], F32, name="d_neg")
         ident = keep.tile([P, P], F32, name="ident")
         warm = keep.tile([P, 1], F32, name="warm")
 
-        nc.scalar.dma_start(out=d_rows[:], in_=demand.rearrange("c (h i) -> (c h) i", h=PASSES))
-        nc.vector.memset(ks_first[:].bitcast(I32), 0)
+        nc.scalar.dma_start(out=d_raw[:], in_=demand.rearrange("c (h p t) -> p (c h) t", h=PASSES, t=PACK))
+        nc.vector.memset(ks_raw[0][:].bitcast(I32), 0)
         nc.vector.memset(warm[:], 0.0)
-        nc.vector.memset(d_neg[:], 0.0)
-        nc.vector.memset(ks_rest[:].bitcast(I32), 0)
+        nc.vector.memset(ks_raw[1][:].bitcast(I32), 0)
+        for c in range(G):
+            if c % STACK:
+                nc.vector.memset(k_scales[c][:].bitcast(I32), 0)
         make_identity(nc, ident[:])
         nc.gpsimd.memset(r_scales[:].bitcast(I32), 0)
         nc.scalar.activation(out=warm[:], in_=warm[:], func=ACT.Exp)
 
-        load_x(0, 0)
+        load_x(0)
+        load_kern_scales(0)
         load_kern(0)
-        load_scale_rows(ks_first, kern_scales[0:1])
-        load_x(0, 1)
+        load_x(1)
         load_kern(1)
-        load_x(1, 0)
-        load_scale_rows(r_scales, read_scales)
+        load_x(2)
+        load_x(3)
+        load_read_scales(0)
         load_read(0)
-        load_scale_rows(ks_rest, kern_scales[1:G])
-        load_x(1, 1)
         load_kern(2)
-        load_x(2, 0)
-        load_read(1)
-        load_x(2, 1)
+        load_x(4)
 
-        def transpose_x(half):
-            bank = psum.tile([P, 2, 2, P], F32, name="x_bank", tag="x_bank", bufs=2)
-            for b in range(2):
-                words = x_raw[half][:, b, :].bitcast(F32)
+        def transpose_x(s, tiles):
+            n = tiles.stop - tiles.start
+            bank = psum.tile([P, n, 2, P], F32, name="x_bank", tag="x_bank", bufs=2)
+            for b in range(n):
+                words = x_raw[s][:, tiles.start + b, :].bitcast(F32)
                 for u in range(2):
                     nc.tensor.transpose(bank[:, b, u, :], words[:, u : J // 2 : 2], ident[:])
-            x_bank[half] = bank
+            x_bank[s, tiles.start] = bank
 
-        def copy_x(half):
-            t = work.tile([P, 2, P, 2], F32, name="x_group", tag="x_group", bufs=2, align_bytes=64)
-            nc.scalar.copy(out=t[:], in_=x_bank[half][:].rearrange("p b u n -> p b n u"))
-            x_group[half] = t
+        def copy_x(s, tiles):
+            n = tiles.stop - tiles.start
+            t = work.tile([P, n, P, 2], F32, name="x_group", tag="x_group", bufs=3, align_bytes=64)
+            nc.scalar.copy(out=t[:], in_=x_bank[s, tiles.start][:].rearrange("p b u n -> p b n u"))
+            x_group[s, tiles.start] = t
 
-        def quantize_x(half):
-            codes = work.tile([P, 2 * P], U32, name="x_codes", tag="x_codes", bufs=3, align_bytes=64)
-            scales = work.tile([P, 2 * P], U8, name="x_scales", tag="x_scales", bufs=3, align_bytes=64)
+        def quantize_x(s, tiles):
+            n = tiles.stop - tiles.start
+            codes = work.tile([P, n * P], U32, name="x_codes", tag="x_codes", bufs=5, align_bytes=64)
+            scales = work.tile([P, n * P], U8, name="x_scales", tag="x_scales", bufs=5, align_bytes=64)
             nc.vector.quantize_mx(
                 out=codes[:].bitcast(FP8X4),
                 scales=scales[:],
-                in_=x_group[half][:].rearrange("p b n u -> p (b n u)").bitcast(BF16),
+                in_=x_group[s, tiles.start][:].rearrange("p b n u -> p (b n u)").bitcast(BF16),
             )
-            x_codes[half], x_scales[half] = codes, scales
+            for b in range(n):
+                cols = slice(b * P, (b + 1) * P)
+                x_codes[s, tiles.start + b], x_scales[s, tiles.start + b] = codes[:, cols], scales[:, cols]
 
-        def sort_kern_words(c, h):
-            t = keep.tile([P, PACK, 2 * P], U8, name="k_words_%d_%d" % (c, h), align_bytes=64)
+        def sort_kern_words(n):
+            c, h = divmod(n, PASSES)
+            t = keep.tile([P, PACK, 2 * P], U8, name="k_words_%d" % n, align_bytes=64)
             nc.vector.tensor_copy(
                 out=t[:].rearrange("p t (a m y) -> p a t m y", m=8, y=2),
                 in_=k_raw[c][:, 1024 * h : 1024 * (h + 1)].rearrange("p (a m t y) -> p a t m y", m=8, t=PACK, y=2),
             )
             k_words[c, h] = t
 
-        def sort_kern_scales(c, h):
-            raw = ks_first[:, 0, :] if c == 0 else ks_rest[:, c - 1, :]
-            t = keep.tile([P, PACK, P], U8, name="k_scales_%d_%d" % (c, h), align_bytes=64)
-            nc.vector.tensor_copy(
-                out=t[:], in_=raw[:, 512 * h : 512 * (h + 1)].rearrange("p (m t) -> p t m", t=PACK)
-            )
-            k_scales[c, h] = t
-
-        def first_matmul(s, h):
-            c, b = divmod(s, TILES)
-            half, cols = s // 2, slice((s % 2) * P, (s % 2 + 1) * P)
-            bank = psum.tile([P, PACK, P], F32, name="acc1", tag="acc1", bufs=3)
+        def first_matmul(s, h, b):
+            c = s // 2
+            bank = psum.tile([P, PACK, P], F32, name="acc1", tag="acc1", bufs=4)
             for t in range(PACK):
+                at = (PACK * h + t) * P
                 nc.tensor.matmul_mx(
                     out=bank[:, t, :],
                     lhsT=k_words[c, h][:, t, :].bitcast(FP4X4),
-                    lhsT_scale=k_scales[c, h][:, t, :],
-                    rhs=x_codes[half][:, cols].bitcast(FP8X4),
-                    rhs_scale=x_scales[half][:, cols],
+                    lhsT_scale=k_scales[c][:, at : at + P],
+                    rhs=x_codes[s, b].bitcast(FP8X4),
+                    rhs_scale=x_scales[s, b],
                     start=True,
                     stop=True,
                 )
-            return bank
+            acc1[s, h, b] = bank
 
-        def exponential(s, h, bank):
-            t = work.tile([P, P, PACK], F32, name="busy", tag="busy", bufs=6)
-            nc.scalar.activation(out=t[:], in_=bank[:].rearrange("p t n -> p n t"), func=ACT.Exp)
-            busy[s, h] = t
+        def exponential(s, h, b):
+            if b == 0:
+                busy[s, h] = work.tile([P, 2, P, PACK], F32, name="busy", tag="busy", bufs=4)
+            nc.scalar.activation(out=busy[s, h][:, b], in_=acc1[s, h, b][:].rearrange("p t n -> p n t"), func=ACT.Exp)
 
-        def cover(s, h):
+        def cover(s, h, tiles):
+            plans = (tiles.stop - tiles.start) * P
             if h == 0:
-                covered[s] = work.tile([P, PASSES, P, PACK], BF16, name="covered", tag="covered", bufs=3, align_bytes=64)
-            row = PASSES * (s // TILES) + h
+                covered[s, tiles.start] = work.tile(
+                    [P, PASSES, plans, PACK], BF16, name="covered", tag="covered", bufs=3, align_bytes=64
+                )
+            row = PASSES * (s // 2) + h
             nc.vector.scalar_tensor_tensor(
-                out=covered[s][:, h],
-                in0=busy[s, h][:],
+                out=covered[s, tiles.start][:, h],
+                in0=busy[s, h][:, tiles].rearrange("p b n t -> p (b n) t"),
                 scalar=1.0,
-                in1=d_bank[:, row : row + 1, :].to_broadcast([P, P, PACK]),
+                in1=d_neg[:, row : row + 1, :].to_broadcast([P, plans, PACK]),
                 op0=ALU.subtract,
                 op1=ALU.mult,
             )
 
-        def quantize_covered(s):
-            codes = work.tile([P, PASSES * P], U32, name="c_codes", tag="c_codes", bufs=3, align_bytes=64)
-            scales = work.tile([P, PASSES * P], U8, name="c_scales", tag="c_scales", bufs=3, align_bytes=64)
+        def quantize_covered(s, tiles, passes):
+            plans = (tiles.stop - tiles.start) * P
+            n = passes.stop - passes.start
+            codes = work.tile([P, n, plans], U32, name="c_codes", tag="c_codes", bufs=4, align_bytes=64)
+            scales = work.tile([P, n, plans], U8, name="c_scales", tag="c_scales", bufs=4, align_bytes=64)
             nc.vector.quantize_mx(
-                out=codes[:].bitcast(FP8X4),
-                scales=scales[:],
-                in_=covered[s][:].rearrange("p h n t -> p (h n t)"),
+                out=codes[:].rearrange("p h n -> p (h n)").bitcast(FP8X4),
+                scales=scales[:].rearrange("p h n -> p (h n)"),
+                in_=covered[s, tiles.start][:, passes].rearrange("p h n t -> p (h n t)"),
             )
-            c_codes[s], c_scales[s] = codes, scales
+            for b in range(tiles.start, tiles.stop):
+                cols = slice((b - tiles.start) * P, (b - tiles.start + 1) * P)
+                for h in range(n):
+                    c_codes[s, b, passes.start + h] = codes[:, h, cols]
+                    c_scales[s, b, passes.start + h] = scales[:, h, cols]
 
-        def second_matmul(s):
-            c = s // TILES
-            bank = psum.tile([P, R], F32, name="acc2", tag="acc2", bufs=2)
-            for h in range(PASSES):
+        def second_matmul(s, b, passes, tag="acc2"):
+            c = s // 2
+            if passes.start == 0:
+                acc2[s, b] = psum.tile([P, R], F32, name=tag, tag=tag, bufs=2)
+            for h in range(passes.start, passes.stop):
                 nc.tensor.matmul_mx(
-                    out=bank[:],
-                    lhsT=c_codes[s][:, h * P : (h + 1) * P].bitcast(FP8X4),
-                    lhsT_scale=c_scales[s][:, h * P : (h + 1) * P],
+                    out=acc2[s, b][:],
+                    lhsT=c_codes[s, b, h].bitcast(FP8X4),
+                    lhsT_scale=c_scales[s, b, h],
                     rhs=r_words[c][:, h, :].bitcast(FP4X4),
                     rhs_scale=r_scales[:, PASSES * c + h, :],
                     start=(h == 0),
                     stop=(h == PASSES - 1),
                 )
-            acc2[s] = bank
 
-        def store(s):
-            c, b = divmod(s, TILES)
-            t = work.tile([P, R], F32, name="result", tag="result", bufs=4)
-            nc.scalar.copy(out=t[:], in_=acc2[s][:])
-            nc.sync.dma_start(out=out[c].rearrange("(p b) r -> p b r", b=TILES)[:, b, :], in_=t[:])
+        def copy_out(s, b, on_vector=False):
+            if b == 0:
+                result[s] = work.tile([P, 2, R], F32, name="result", tag="result", bufs=3)
+            if on_vector:
+                nc.vector.tensor_copy(out=result[s][:, b, :], in_=acc2[s, b][:])
+            else:
+                nc.scalar.copy(out=result[s][:, b, :], in_=acc2[s, b][:])
 
-        transpose_x(0)
-        copy_x(0)
-        sort_kern_words(0, 0)
-        sort_kern_scales(0, 0)
-        quantize_x(0)
-        nc.vector.tensor_scalar(
-            out=d_neg[0 : G * PASSES, :], in0=d_rows[:], scalar1=-1.0, scalar2=None, op0=ALU.mult
-        )
-        d_bank = psum.tile([P, P, PACK], F32, name="d_bank", tag="d_bank", bufs=1)
-        sort_kern_words(0, 1)
-        sort_kern_scales(0, 1)
-        transpose_x(1)
-        copy_x(1)
-        sort_kern_words(1, 0)
+        def store(s, tiles):
+            c, k = divmod(s, 2)
+            rows = out[c].rearrange("(p b) r -> p b r", b=TILES)[:, 2 * k : 2 * k + 2, :]
+            nc.sync.dma_start(out=rows[:, tiles, :], in_=result[s][:, tiles, :])
 
-        for s in range(STEPS + 3):
-            c, b = divmod(s, TILES)
-            if s < STEPS:
-                bank0 = first_matmul(s, 0)
-            if s >= 3:
-                second_matmul(s - 3)
-                store(s - 3)
-            if s < STEPS:
-                exponential(s, 0, bank0)
-                bank1 = first_matmul(s, 1)
-                if s == 0:
-                    for t in range(PACK):
-                        nc.tensor.transpose(d_bank[:, :, t], d_neg[:, t:512:PACK], ident[:])
-                if s % 2 == 1 and (s + 3) // 2 < 2 * G:
-                    copy_x((s + 3) // 2)
-                exponential(s, 1, bank1)
-                if s % 2 == 0 and (s + 4) // 2 < 2 * G:
-                    transpose_x((s + 4) // 2)
-            if 1 <= s <= STEPS:
-                cover(s - 1, 0)
-            if 2 <= s <= STEPS + 1:
-                quantize_covered(s - 2)
-            if 1 <= s <= STEPS:
-                cover(s - 1, 1)
-            if s % 2 == 0 and (s + 2) // 2 < 2 * G:
-                quantize_x((s + 2) // 2)
-            if b % 2 == 0 and c + 1 < G:
-                sort_kern_scales(c + 1, b // 2)
-            if b == 1 and c + 1 < G:
-                sort_kern_words(c + 1, 1)
-            if b == 3 and c + 2 < G:
-                sort_kern_words(c + 2, 0)
-            if c + 3 < G:
-                if b == 0:
-                    load_kern(c + 3)
-                if b == 1:
-                    load_x(c + 3, 0)
-                if b == 3:
-                    load_x(c + 3, 1)
-            if b == 2 and c + 2 < G:
-                load_read(c + 2)
+        both, first, second = slice(0, 2), slice(0, 1), slice(1, 2)
+
+        transpose_x(0, first)
+        copy_x(0, first)
+        transpose_x(0, second)
+        copy_x(0, second)
+        sort_kern_scales(0)
+        sort_kern_words(0)
+        quantize_x(0, first)
+        quantize_x(0, second)
+        sort_kern_words(1)
+        nc.vector.tensor_scalar(out=d_neg[:], in0=d_raw[:], scalar1=-1.0, scalar2=None, op0=ALU.mult)
+        transpose_x(1, both)
+        copy_x(1, both)
+        sort_kern_words(2)
+        quantize_x(1, both)
+        sort_kern_words(3)
+        shift_kern_scales(1)
+
+        last = STEPS - 1
+        for s in range(last):
+            c, k = divmod(s, 2)
+            if k == 1 and c + 3 < G:
+                load_kern(c + 3)
+            if s + 5 < STEPS:
+                load_x(s + 5)
+            if k == 0 and c + 1 < G:
+                load_read(c + 1)
+            if s in (1, 5):
+                load_read_scales(c + 2)
+            if s == 0:
+                load_kern_scales(1)
+            if k == 1 and c + 2 < G and (c + 2) % STACK:
+                shift_kern_scales(c + 2)
+            first_matmul(s, 0, 0)
+            first_matmul(s, 0, 1)
+            exponential(s, 0, 0)
+            exponential(s, 0, 1)
+            if s >= 2:
+                second_matmul(s - 2, 0, both)
+                copy_out(s - 2, 0)
+                store(s - 2, first)
+            if s == 0:
+                transpose_x(2, both)
+                copy_x(2, both)
+            first_matmul(s, 1, 0)
+            if s >= 2:
+                second_matmul(s - 2, 1, both)
+            first_matmul(s, 1, 1)
+            if k == 0:
+                for ahead in (s + 3, s + 4):
+                    if ahead < STEPS:
+                        transpose_x(ahead, both)
+            exponential(s, 1, 0)
+            exponential(s, 1, 1)
+            if s + 3 < STEPS:
+                copy_x(s + 3, both)
+            if s >= 2:
+                copy_out(s - 2, 1)
+                store(s - 2, second)
+
+            cover(s, 0, both)
+            if s >= 1:
+                quantize_covered(s - 1, both, both)
+            if s + 2 < STEPS:
+                quantize_x(s + 2, both)
+            cover(s, 1, both)
+            if s + 4 < STEPS:
+                sort_kern_words(s + 4)
+            if s == 3:
+                sort_kern_scales(1)
+
+        s = last
+        first_matmul(s, 0, 0)
+        first_matmul(s, 1, 0)
+        exponential(s, 0, 0)
+        exponential(s, 1, 0)
+        second_matmul(s - 2, 0, both)
+        copy_out(s - 2, 0)
+        store(s - 2, first)
+        first_matmul(s, 0, 1)
+        first_matmul(s, 1, 1)
+        second_matmul(s - 2, 1, both)
+        exponential(s, 0, 1)
+        exponential(s, 1, 1)
+        copy_out(s - 2, 1)
+        store(s - 2, second)
+        cover(s, 0, first)
+        quantize_covered(s - 1, both, both)
+        second_matmul(s - 1, 0, both, "x_bank")
+        second_matmul(s - 1, 1, both, "x_bank")
+        cover(s, 1, first)
+        cover(s, 0, second)
+        quantize_covered(s, first, both)
+        quantize_covered(s, second, first)
+        copy_out(s - 1, 0)
+        store(s - 1, first)
+        copy_out(s - 1, 1)
+        store(s - 1, second)
+        second_matmul(s, 0, both)
+        second_matmul(s, 1, first)
+        cover(s, 1, second)
+        quantize_covered(s, second, second)
+        second_matmul(s, 1, second)
+        copy_out(s, 0)
+        store(s, first)
+        copy_out(s, 1, True)
+        store(s, second)

@@ -3,8 +3,8 @@ from contextlib import ExitStack
 import concourse.mybir as mybir
 from concourse.masks import make_identity
 
-G, PLANS, J, I, R = 6, 512, 512, 1024, 512
-FLOPS = 2 * G * PLANS * (J * I + I * R)
+PERIODS, PLANS, STATIONS, ZONES, READOUTS = 6, 512, 512, 1024, 512
+FLOPS = 2 * PERIODS * PLANS * (STATIONS * ZONES + ZONES * READOUTS)
 
 F32 = mybir.dt.float32
 BF16 = mybir.dt.bfloat16
@@ -17,11 +17,20 @@ ALU = mybir.AluOpType
 ACT = mybir.ActivationFunctionType
 
 P = 128
-PACK = 4
+SLOTS = 4
+QUADRANTS = 4
 TILES = PLANS // P
-PASSES = I // 512
-STEPS = 2 * G
+PASSES = ZONES // (P * SLOTS)
+STEPS = PERIODS * TILES // 2
 STACK = 4
+
+LOAD_AHEAD = 5
+TURN_AHEAD = 2
+SORT_AHEAD = 5
+OUT_BEHIND = 2
+VECTOR_OUT_FROM = 8
+
+BOTH, FIRST, SECOND = slice(0, 2), slice(0, 1), slice(1, 2)
 
 
 def tile_ambulance_expected_coverage_s14_kernel(
@@ -34,111 +43,96 @@ def tile_ambulance_expected_coverage_s14_kernel(
         psum = ctx.enter_context(tc.psum_pool(name="psum", bufs=2))
         ctx.enter_context(tc.manual_schedule())
 
-        x_raw, k_raw, r_words = {}, {}, {}
-        x_bank, x_group, x_codes, x_scales = {}, {}, {}, {}
-        k_words, k_scales, k_sorted = {}, {}, {}
-        acc1, busy, covered, c_codes, c_scales, acc2, result = {}, {}, {}, {}, {}, {}, {}
+        x_rows, x_bank, x_group, x_codes, x_scales = {}, {}, {}, {}, {}
+        k_raw, k_words, k_scales, ks_sorted, r_words = {}, {}, {}, {}, {}
+        logbusy, busy, covered, c_codes, c_scales, sums, result = {}, {}, {}, {}, {}, {}, {}
+
+        ks_raw = [keep.tile([P, ZONES], U8, name="ks_raw_%d" % n, align_bytes=64) for n in range(2)]
+        shifted = [c for c in range(PERIODS) if c % STACK]
+        for c in shifted:
+            k_scales[c] = keep.tile([P, ZONES], U8, name="k_scales_%d" % c, align_bytes=64)
+        r_scales = keep.tile([P, PERIODS * PASSES, READOUTS], U8, name="r_scales", align_bytes=64)
+        d_raw = keep.tile([P, PERIODS * PASSES, SLOTS], BF16, name="d_raw")
+        d_neg = keep.tile([P, PERIODS * PASSES, SLOTS], F32, name="d_neg")
+        ident = keep.tile([P, P], F32, name="ident")
+
+        def plan_rows(array, s):
+            c, half = divmod(s, 2)
+            return array[c].rearrange("(p b) n -> p b n", b=TILES)[:, 2 * half : 2 * half + 2, :]
 
         def load_x(s):
-            c, k = divmod(s, 2)
-            t = keep.tile([P, 2, J], BF16, name="x_raw_%d" % s)
-            nc.sync.dma_start(out=t[:], in_=load[c].rearrange("(p b) j -> p b j", b=TILES)[:, 2 * k : 2 * k + 2, :])
-            x_raw[s] = t
+            x_rows[s] = keep.tile([P, 2, STATIONS], BF16, name="x_rows_%d" % s)
+            nc.sync.dma_start(out=x_rows[s][:], in_=plan_rows(load, s))
 
         def load_kern(c):
-            t = keep.tile([P, 2 * I], U8, name="k_raw_%d" % c, align_bytes=64)
-            nc.sync.dma_start(out=t[:].bitcast(I32), in_=kern_words[c].bitcast(I32))
-            k_raw[c] = t
+            k_raw[c] = keep.tile([P, 2 * ZONES], U8, name="k_raw_%d" % c, align_bytes=64)
+            nc.sync.dma_start(out=k_raw[c][:].bitcast(I32), in_=kern_words[c].bitcast(I32))
 
         def load_read(c):
-            t = keep.tile([P, PASSES, 2 * R], U8, name="r_words_%d" % c, align_bytes=64)
+            r_words[c] = keep.tile([P, PASSES, 2 * READOUTS], U8, name="r_words_%d" % c, align_bytes=64)
             nc.sync.dma_start(
-                out=t[:].bitcast(I32),
+                out=r_words[c][:].bitcast(I32),
                 in_=read_words[PASSES * c : PASSES * (c + 1)].rearrange("h p n -> p h n").bitcast(I32),
             )
-            r_words[c] = t
 
         def load_read_scales(c):
-            rows = slice(PASSES * c, PASSES * (c + 2))
-            for q in range(4):
+            passes = slice(PASSES * c, PASSES * (c + 2))
+            for q in range(QUADRANTS):
                 nc.sync.dma_start(
-                    out=r_scales[32 * q : 32 * q + 4, rows, :].bitcast(I32),
-                    in_=read_scales[rows, 4 * q : 4 * q + 4, :].rearrange("g r n -> r g n").bitcast(I32),
+                    out=r_scales[32 * q : 32 * q + 4, passes, :].bitcast(I32),
+                    in_=read_scales[passes, 4 * q : 4 * q + 4, :].rearrange("g r n -> r g n").bitcast(I32),
                 )
 
         def load_kern_scales(stack):
-            first = STACK * stack
-            n = min(STACK, G - first)
-            for q in range(4):
+            lowest = STACK * stack
+            levels = min(STACK, PERIODS - lowest)
+            for q in range(QUADRANTS):
                 nc.sync.dma_start(
-                    out=ks_raw[stack][32 * q : 32 * q + 4 * n, :].bitcast(I32),
-                    in_=kern_scales[first : first + n, 4 * q : 4 * q + 4, :].bitcast(I32),
+                    out=ks_raw[stack][32 * q : 32 * q + 4 * levels, :].bitcast(I32),
+                    in_=kern_scales[lowest : lowest + levels, 4 * q : 4 * q + 4, :].bitcast(I32),
                 )
 
-        def sort_kern_scales(stack):
-            t = keep.tile([P, I], U8, name="ks_sorted_%d" % stack, align_bytes=64)
+        def sort_kern_words(n):
+            c, h = divmod(n, PASSES)
+            k_words[c, h] = keep.tile([P, SLOTS, 2 * P], U8, name="k_words_%d" % n, align_bytes=64)
+            raw = k_raw[c][:, h * ZONES : (h + 1) * ZONES]
             nc.vector.tensor_copy(
-                out=t[:].rearrange("p (h t m) -> p h t m", h=PASSES, t=PACK),
-                in_=ks_raw[stack][:].rearrange("p (h m t) -> p h t m", h=PASSES, t=PACK),
+                out=k_words[c, h][:].rearrange("p t (a m y) -> p a t m y", m=8, y=2),
+                in_=raw.rearrange("p (a m t y) -> p a t m y", m=8, t=SLOTS, y=2),
             )
-            k_sorted[stack] = t
-            k_scales[STACK * stack] = t
+
+        def sort_kern_scales(stack, passes):
+            if passes.start == 0:
+                ks_sorted[stack] = keep.tile([P, ZONES], U8, name="ks_sorted_%d" % stack, align_bytes=64)
+                k_scales[STACK * stack] = ks_sorted[stack]
+            nc.vector.tensor_copy(
+                out=ks_sorted[stack][:].rearrange("p (h t m) -> p h t m", h=PASSES, t=SLOTS)[:, passes],
+                in_=ks_raw[stack][:].rearrange("p (h m t) -> p h t m", h=PASSES, t=SLOTS)[:, passes],
+            )
 
         def shift_kern_scales(c):
             stack, level = divmod(c, STACK)
-            for q in range(4):
+            for q in range(QUADRANTS):
+                at = 32 * q + 4 * level
                 nc.sync.dma_start(
                     out=k_scales[c][32 * q : 32 * q + 4, :].bitcast(I32),
-                    in_=k_sorted[stack][32 * q + 4 * level : 32 * q + 4 * level + 4, :].bitcast(I32),
+                    in_=ks_sorted[stack][at : at + 4, :].bitcast(I32),
                 )
 
-        ks_raw = [keep.tile([P, I], U8, name="ks_raw_%d" % n, align_bytes=64) for n in range(2)]
-        for c in range(G):
-            if c % STACK:
-                k_scales[c] = keep.tile([P, I], U8, name="k_scales_%d" % c, align_bytes=64)
-        r_scales = keep.tile([P, G * PASSES, R], U8, name="r_scales", align_bytes=64)
-        d_raw = keep.tile([P, G * PASSES, PACK], BF16, name="d_raw")
-        d_neg = keep.tile([P, G * PASSES, PACK], F32, name="d_neg")
-        ident = keep.tile([P, P], F32, name="ident")
-        warm = keep.tile([P, 1], F32, name="warm")
-
-        nc.scalar.dma_start(out=d_raw[:], in_=demand.rearrange("c (h p t) -> p (c h) t", h=PASSES, t=PACK))
-        nc.vector.memset(ks_raw[0][:].bitcast(I32), 0)
-        nc.vector.memset(warm[:], 0.0)
-        nc.vector.memset(ks_raw[1][:].bitcast(I32), 0)
-        for c in range(G):
-            if c % STACK:
-                nc.vector.memset(k_scales[c][:].bitcast(I32), 0)
-        make_identity(nc, ident[:])
-        nc.gpsimd.memset(r_scales[:].bitcast(I32), 0)
-        nc.scalar.activation(out=warm[:], in_=warm[:], func=ACT.Exp)
-
-        load_x(0)
-        load_kern_scales(0)
-        load_kern(0)
-        load_x(1)
-        load_kern(1)
-        load_x(2)
-        load_x(3)
-        load_read_scales(0)
-        load_read(0)
-        load_kern(2)
-        load_x(4)
-
-        def transpose_x(s, tiles):
+        def transpose_x(s, tiles, tag="x_bank"):
             n = tiles.stop - tiles.start
-            bank = psum.tile([P, n, 2, P], F32, name="x_bank", tag="x_bank", bufs=2)
+            bank = psum.tile([P, n, 2, P], F32, name=tag, tag=tag, bufs=2)
             for b in range(n):
-                words = x_raw[s][:, tiles.start + b, :].bitcast(F32)
+                words = x_rows[s][:, tiles.start + b, :].bitcast(F32)
                 for u in range(2):
-                    nc.tensor.transpose(bank[:, b, u, :], words[:, u : J // 2 : 2], ident[:])
+                    nc.tensor.transpose(bank[:, b, u, :], words[:, u : STATIONS // 2 : 2], ident[:])
             x_bank[s, tiles.start] = bank
 
         def copy_x(s, tiles):
             n = tiles.stop - tiles.start
-            t = work.tile([P, n, P, 2], F32, name="x_group", tag="x_group", bufs=3, align_bytes=64)
-            nc.scalar.copy(out=t[:], in_=x_bank[s, tiles.start][:].rearrange("p b u n -> p b n u"))
-            x_group[s, tiles.start] = t
+            group = work.tile([P, n, P, 2], F32, name="x_group", tag="x_group", bufs=3, align_bytes=64)
+            nc.scalar.copy(out=group[:], in_=x_bank[s, tiles.start][:].rearrange("p b u n -> p b n u"))
+            x_group[s, tiles.start] = group
 
         def quantize_x(s, tiles):
             n = tiles.stop - tiles.start
@@ -150,23 +144,14 @@ def tile_ambulance_expected_coverage_s14_kernel(
                 in_=x_group[s, tiles.start][:].rearrange("p b n u -> p (b n u)").bitcast(BF16),
             )
             for b in range(n):
-                cols = slice(b * P, (b + 1) * P)
-                x_codes[s, tiles.start + b], x_scales[s, tiles.start + b] = codes[:, cols], scales[:, cols]
-
-        def sort_kern_words(n):
-            c, h = divmod(n, PASSES)
-            t = keep.tile([P, PACK, 2 * P], U8, name="k_words_%d" % n, align_bytes=64)
-            nc.vector.tensor_copy(
-                out=t[:].rearrange("p t (a m y) -> p a t m y", m=8, y=2),
-                in_=k_raw[c][:, 1024 * h : 1024 * (h + 1)].rearrange("p (a m t y) -> p a t m y", m=8, t=PACK, y=2),
-            )
-            k_words[c, h] = t
+                plans = slice(b * P, (b + 1) * P)
+                x_codes[s, tiles.start + b], x_scales[s, tiles.start + b] = codes[:, plans], scales[:, plans]
 
         def first_matmul(s, h, b):
             c = s // 2
-            bank = psum.tile([P, PACK, P], F32, name="acc1", tag="acc1", bufs=4)
-            for t in range(PACK):
-                at = (PACK * h + t) * P
+            bank = psum.tile([P, SLOTS, P], F32, name="logbusy", tag="logbusy", bufs=4)
+            for t in range(SLOTS):
+                at = (SLOTS * h + t) * P
                 nc.tensor.matmul_mx(
                     out=bank[:, t, :],
                     lhsT=k_words[c, h][:, t, :].bitcast(FP4X4),
@@ -176,25 +161,27 @@ def tile_ambulance_expected_coverage_s14_kernel(
                     start=True,
                     stop=True,
                 )
-            acc1[s, h, b] = bank
+            logbusy[s, h, b] = bank
 
         def exponential(s, h, b):
             if b == 0:
-                busy[s, h] = work.tile([P, 2, P, PACK], F32, name="busy", tag="busy", bufs=4)
-            nc.scalar.activation(out=busy[s, h][:, b], in_=acc1[s, h, b][:].rearrange("p t n -> p n t"), func=ACT.Exp)
+                busy[s, h] = work.tile([P, 2, P, SLOTS], F32, name="busy", tag="busy", bufs=4)
+            nc.scalar.activation(
+                out=busy[s, h][:, b], in_=logbusy[s, h, b][:].rearrange("p t n -> p n t"), func=ACT.Exp
+            )
 
         def cover(s, h, tiles):
             plans = (tiles.stop - tiles.start) * P
             if h == 0:
                 covered[s, tiles.start] = work.tile(
-                    [P, PASSES, plans, PACK], BF16, name="covered", tag="covered", bufs=3, align_bytes=64
+                    [P, PASSES, plans, SLOTS], BF16, name="covered", tag="covered", bufs=3, align_bytes=64
                 )
             row = PASSES * (s // 2) + h
             nc.vector.scalar_tensor_tensor(
                 out=covered[s, tiles.start][:, h],
                 in0=busy[s, h][:, tiles].rearrange("p b n t -> p (b n) t"),
                 scalar=1.0,
-                in1=d_neg[:, row : row + 1, :].to_broadcast([P, plans, PACK]),
+                in1=d_neg[:, row : row + 1, :].to_broadcast([P, plans, SLOTS]),
                 op0=ALU.subtract,
                 op1=ALU.mult,
             )
@@ -215,139 +202,154 @@ def tile_ambulance_expected_coverage_s14_kernel(
                     c_codes[s, b, passes.start + h] = codes[:, h, cols]
                     c_scales[s, b, passes.start + h] = scales[:, h, cols]
 
-        def second_matmul(s, b, passes, tag="acc2"):
+        def second_pass(bank, s, b, h, readouts):
             c = s // 2
-            if passes.start == 0:
-                acc2[s, b] = psum.tile([P, R], F32, name=tag, tag=tag, bufs=2)
-            for h in range(passes.start, passes.stop):
-                nc.tensor.matmul_mx(
-                    out=acc2[s, b][:],
-                    lhsT=c_codes[s, b, h].bitcast(FP8X4),
-                    lhsT_scale=c_scales[s, b, h],
-                    rhs=r_words[c][:, h, :].bitcast(FP4X4),
-                    rhs_scale=r_scales[:, PASSES * c + h, :],
-                    start=(h == 0),
-                    stop=(h == PASSES - 1),
-                )
+            nc.tensor.matmul_mx(
+                out=bank[:],
+                lhsT=c_codes[s, b, h].bitcast(FP8X4),
+                lhsT_scale=c_scales[s, b, h],
+                rhs=r_words[c][:, h, 2 * readouts.start : 2 * readouts.stop].bitcast(FP4X4),
+                rhs_scale=r_scales[:, PASSES * c + h, readouts],
+                start=(h == 0),
+                stop=(h == PASSES - 1),
+            )
 
-        def copy_out(s, b, on_vector=False):
+        def second_matmul(s, b, tag="sums"):
+            sums[s, b] = psum.tile([P, READOUTS], F32, name=tag, tag=tag, bufs=2)
+            for h in range(PASSES):
+                second_pass(sums[s, b], s, b, h, slice(0, READOUTS))
+
+        def store(s, b, copy=nc.scalar.copy):
             if b == 0:
-                result[s] = work.tile([P, 2, R], F32, name="result", tag="result", bufs=3)
-            if on_vector:
-                nc.vector.tensor_copy(out=result[s][:, b, :], in_=acc2[s, b][:])
-            else:
-                nc.scalar.copy(out=result[s][:, b, :], in_=acc2[s, b][:])
+                result[s] = work.tile([P, 2, READOUTS], F32, name="result", tag="result", bufs=3)
+            copy(out=result[s][:, b, :], in_=sums[s, b][:])
+            nc.sync.dma_start(out=plan_rows(out, s)[:, b : b + 1, :], in_=result[s][:, b : b + 1, :])
 
-        def store(s, tiles):
-            c, k = divmod(s, 2)
-            rows = out[c].rearrange("(p b) r -> p b r", b=TILES)[:, 2 * k : 2 * k + 2, :]
-            nc.sync.dma_start(out=rows[:, tiles, :], in_=result[s][:, tiles, :])
+        nc.vector.memset(ks_raw[0][:].bitcast(I32), 0)
+        nc.vector.memset(ks_raw[1][:].bitcast(I32), 0)
+        for c in shifted:
+            nc.vector.memset(k_scales[c][:].bitcast(I32), 0)
+        make_identity(nc, ident[:])
+        nc.gpsimd.memset(r_scales[:].bitcast(I32), 0)
 
-        both, first, second = slice(0, 2), slice(0, 1), slice(1, 2)
+        load_x(0)
+        load_kern(0)
+        load_kern_scales(0)
+        load_x(1)
+        load_kern(1)
+        nc.sync.dma_start(out=d_raw[:], in_=demand.rearrange("c (h p t) -> p (c h) t", h=PASSES, t=SLOTS))
+        load_kern(2)
+        load_x(2)
+        load_x(3)
+        load_read_scales(0)
+        load_read(0)
+        load_x(4)
 
-        transpose_x(0, first)
-        copy_x(0, first)
-        transpose_x(0, second)
-        copy_x(0, second)
-        sort_kern_scales(0)
+        for tile in (FIRST, SECOND):
+            transpose_x(0, tile)
+            copy_x(0, tile)
         sort_kern_words(0)
-        quantize_x(0, first)
-        quantize_x(0, second)
+        sort_kern_scales(0, FIRST)
+        quantize_x(0, FIRST)
+        quantize_x(0, SECOND)
+        sort_kern_scales(0, SECOND)
         sort_kern_words(1)
-        nc.vector.tensor_scalar(out=d_neg[:], in0=d_raw[:], scalar1=-1.0, scalar2=None, op0=ALU.mult)
-        transpose_x(1, both)
-        copy_x(1, both)
+        transpose_x(1, BOTH, "sums")
+        copy_x(1, BOTH)
         sort_kern_words(2)
-        quantize_x(1, both)
-        sort_kern_words(3)
+        quantize_x(1, BOTH)
+        nc.vector.tensor_scalar(out=d_neg[:], in0=d_raw[:], scalar1=-1.0, scalar2=None, op0=ALU.mult)
+        for n in range(3, SORT_AHEAD):
+            sort_kern_words(n)
         shift_kern_scales(1)
 
         last = STEPS - 1
         for s in range(last):
-            c, k = divmod(s, 2)
-            if k == 1 and c + 3 < G:
+            c, half = divmod(s, 2)
+            turn, behind = s + TURN_AHEAD, s - OUT_BEHIND
+
+            if half == 0 and c + 3 < PERIODS:
                 load_kern(c + 3)
-            if s + 5 < STEPS:
-                load_x(s + 5)
-            if k == 0 and c + 1 < G:
+            if s + LOAD_AHEAD < STEPS:
+                load_x(s + LOAD_AHEAD)
+            if half == 0 and c + 1 < PERIODS:
                 load_read(c + 1)
-            if s in (1, 5):
+            if half == 1 and c % 2 == 0 and c + 2 < PERIODS:
                 load_read_scales(c + 2)
             if s == 0:
                 load_kern_scales(1)
-            if k == 1 and c + 2 < G and (c + 2) % STACK:
+            if half == 1 and c + 2 in shifted:
                 shift_kern_scales(c + 2)
+
             first_matmul(s, 0, 0)
             first_matmul(s, 0, 1)
             exponential(s, 0, 0)
             exponential(s, 0, 1)
-            if s >= 2:
-                second_matmul(s - 2, 0, both)
-                copy_out(s - 2, 0)
-                store(s - 2, first)
-            if s == 0:
-                transpose_x(2, both)
-                copy_x(2, both)
             first_matmul(s, 1, 0)
-            if s >= 2:
-                second_matmul(s - 2, 1, both)
+            if behind >= 0:
+                second_matmul(behind, 0)
+                store(behind, 0, nc.vector.tensor_copy if s >= VECTOR_OUT_FROM else nc.scalar.copy)
             first_matmul(s, 1, 1)
-            if k == 0:
-                for ahead in (s + 3, s + 4):
-                    if ahead < STEPS:
-                        transpose_x(ahead, both)
+            if behind >= 0:
+                second_matmul(behind, 1)
+            if turn < STEPS:
+                transpose_x(turn, BOTH)
             exponential(s, 1, 0)
             exponential(s, 1, 1)
-            if s + 3 < STEPS:
-                copy_x(s + 3, both)
-            if s >= 2:
-                copy_out(s - 2, 1)
-                store(s - 2, second)
+            if turn < STEPS:
+                copy_x(turn, BOTH)
+            if behind >= 0:
+                store(behind, 1)
 
-            cover(s, 0, both)
+            cover(s, 0, BOTH)
             if s >= 1:
-                quantize_covered(s - 1, both, both)
-            if s + 2 < STEPS:
-                quantize_x(s + 2, both)
-            cover(s, 1, both)
-            if s + 4 < STEPS:
-                sort_kern_words(s + 4)
-            if s == 3:
-                sort_kern_scales(1)
+                quantize_covered(s - 1, BOTH, BOTH)
+            cover(s, 1, BOTH)
+            if behind < 0:
+                quantize_x(turn, BOTH)
+            if s + SORT_AHEAD < PERIODS * PASSES:
+                sort_kern_words(s + SORT_AHEAD)
+            if s == STACK - 1:
+                sort_kern_scales(1, BOTH)
+            if behind >= 0 and turn < STEPS:
+                quantize_x(turn, BOTH)
 
-        s = last
-        first_matmul(s, 0, 0)
-        first_matmul(s, 1, 0)
-        exponential(s, 0, 0)
-        exponential(s, 1, 0)
-        second_matmul(s - 2, 0, both)
-        copy_out(s - 2, 0)
-        store(s - 2, first)
-        first_matmul(s, 0, 1)
-        first_matmul(s, 1, 1)
-        second_matmul(s - 2, 1, both)
-        exponential(s, 0, 1)
-        exponential(s, 1, 1)
-        copy_out(s - 2, 1)
-        store(s - 2, second)
-        cover(s, 0, first)
-        quantize_covered(s - 1, both, both)
-        second_matmul(s - 1, 0, both, "x_bank")
-        second_matmul(s - 1, 1, both, "x_bank")
-        cover(s, 1, first)
-        cover(s, 0, second)
-        quantize_covered(s, first, both)
-        quantize_covered(s, second, first)
-        copy_out(s - 1, 0)
-        store(s - 1, first)
-        copy_out(s - 1, 1)
-        store(s - 1, second)
-        second_matmul(s, 0, both)
-        second_matmul(s, 1, first)
-        cover(s, 1, second)
-        quantize_covered(s, second, second)
-        second_matmul(s, 1, second)
-        copy_out(s, 0)
-        store(s, first)
-        copy_out(s, 1, True)
-        store(s, second)
+        behind, before = last - OUT_BEHIND, last - 1
+        first_matmul(last, 0, 0)
+        first_matmul(last, 1, 0)
+        exponential(last, 0, 0)
+        exponential(last, 1, 0)
+        second_matmul(behind, 0)
+        store(behind, 0)
+        first_matmul(last, 0, 1)
+        first_matmul(last, 1, 1)
+        second_matmul(behind, 1)
+        exponential(last, 0, 1)
+        exponential(last, 1, 1)
+        store(behind, 1)
+        cover(last, 0, FIRST)
+        quantize_covered(before, BOTH, BOTH)
+        second_matmul(before, 0, "x_bank")
+        second_matmul(before, 1, "x_bank")
+        cover(last, 1, FIRST)
+        cover(last, 0, SECOND)
+        quantize_covered(last, FIRST, BOTH)
+        quantize_covered(last, SECOND, FIRST)
+        store(before, 0)
+        store(before, 1)
+        second_matmul(last, 0)
+
+        columns = [slice(q * P, (q + 1) * P) for q in range(READOUTS // P)]
+        quarters = [psum.tile([P, P], F32, name="logbusy", tag="logbusy", bufs=4) for cols in columns]
+        for bank, cols in zip(quarters, columns):
+            second_pass(bank, last, 1, 0, cols)
+        cover(last, 1, SECOND)
+        quantize_covered(last, SECOND, SECOND)
+        for bank, cols in zip(quarters, columns):
+            second_pass(bank, last, 1, 1, cols)
+        store(last, 0)
+        for pair, copy in enumerate((nc.vector.tensor_copy, nc.scalar.copy)):
+            for q in (2 * pair, 2 * pair + 1):
+                copy(out=result[last][:, 1, columns[q]], in_=quarters[q][:])
+            both_columns = slice(2 * pair * P, 2 * (pair + 1) * P)
+            nc.sync.dma_start(out=plan_rows(out, last)[:, 1, both_columns], in_=result[last][:, 1, both_columns])

from contextlib import ExitStack

import concourse.mybir as mybir
from concourse.masks import make_identity

PERIODS, PLANS, STATIONS, ZONES, READOUTS = 6, 512, 512, 1024, 512
FLOPS = 2 * PERIODS * PLANS * (STATIONS * ZONES + ZONES * READOUTS)

F32 = mybir.dt.float32
BF16 = mybir.dt.bfloat16
I32 = mybir.dt.int32
U32 = mybir.dt.uint32
U8 = mybir.dt.uint8
FP8X4 = mybir.dt.float8_e4m3fn_x4
FP4X4 = mybir.dt.float4_e2m1fn_x4
ALU = mybir.AluOpType
ACT = mybir.ActivationFunctionType

P = 128
SLOTS = 4
QUADRANTS = 4
TILES = PLANS // P
PASSES = ZONES // (P * SLOTS)
STEPS = PERIODS * TILES // 2
STACK = 4

LOAD_AHEAD = 5
TURN_AHEAD = 2
SORT_AHEAD = 5
OUT_BEHIND = 2
VECTOR_OUT_FROM = 8

BOTH, FIRST, SECOND = slice(0, 2), slice(0, 1), slice(1, 2)


def tile_ambulance_expected_coverage_s14_kernel(
    tc, load, kern_words, kern_scales, demand, read_words, read_scales, out
):
    nc = tc.nc
    with ExitStack() as ctx:
        keep = ctx.enter_context(tc.tile_pool(name="keep", bufs=1))
        work = ctx.enter_context(tc.tile_pool(name="work", bufs=3))
        psum = ctx.enter_context(tc.psum_pool(name="psum", bufs=2))
        ctx.enter_context(tc.manual_schedule())

        x_rows, x_bank, x_group, x_codes, x_scales = {}, {}, {}, {}, {}
        k_raw, k_words, k_scales, ks_sorted, r_words = {}, {}, {}, {}, {}
        logbusy, busy, covered, c_codes, c_scales, sums, result = {}, {}, {}, {}, {}, {}, {}

        ks_raw = [keep.tile([P, ZONES], U8, name="ks_raw_%d" % n, align_bytes=64) for n in range(2)]
        shifted = [c for c in range(PERIODS) if c % STACK]
        for c in shifted:
            k_scales[c] = keep.tile([P, ZONES], U8, name="k_scales_%d" % c, align_bytes=64)
        r_scales = keep.tile([P, PERIODS * PASSES, READOUTS], U8, name="r_scales", align_bytes=64)
        d_raw = keep.tile([P, PERIODS * PASSES, SLOTS], BF16, name="d_raw")
        d_neg = keep.tile([P, PERIODS * PASSES, SLOTS], F32, name="d_neg")
        ident = keep.tile([P, P], F32, name="ident")

        def plan_rows(array, s):
            c, half = divmod(s, 2)
            return array[c].rearrange("(p b) n -> p b n", b=TILES)[:, 2 * half : 2 * half + 2, :]

        def load_x(s):
            x_rows[s] = keep.tile([P, 2, STATIONS], BF16, name="x_rows_%d" % s)
            nc.sync.dma_start(out=x_rows[s][:], in_=plan_rows(load, s))

        def load_kern(c):
            k_raw[c] = keep.tile([P, 2 * ZONES], U8, name="k_raw_%d" % c, align_bytes=64)
            nc.sync.dma_start(out=k_raw[c][:].bitcast(I32), in_=kern_words[c].bitcast(I32))

        def load_read(c):
            r_words[c] = keep.tile([P, PASSES, 2 * READOUTS], U8, name="r_words_%d" % c, align_bytes=64)
            nc.sync.dma_start(
                out=r_words[c][:].bitcast(I32),
                in_=read_words[PASSES * c : PASSES * (c + 1)].rearrange("h p n -> p h n").bitcast(I32),
            )

        def load_read_scales(c):
            passes = slice(PASSES * c, PASSES * (c + 2))
            for q in range(QUADRANTS):
                nc.sync.dma_start(
                    out=r_scales[32 * q : 32 * q + 4, passes, :].bitcast(I32),
                    in_=read_scales[passes, 4 * q : 4 * q + 4, :].rearrange("g r n -> r g n").bitcast(I32),
                )

        def load_kern_scales(stack):
            lowest = STACK * stack
            levels = min(STACK, PERIODS - lowest)
            for q in range(QUADRANTS):
                nc.sync.dma_start(
                    out=ks_raw[stack][32 * q : 32 * q + 4 * levels, :].bitcast(I32),
                    in_=kern_scales[lowest : lowest + levels, 4 * q : 4 * q + 4, :].bitcast(I32),
                )

        def sort_kern_words(n):
            c, h = divmod(n, PASSES)
            k_words[c, h] = keep.tile([P, SLOTS, 2 * P], U8, name="k_words_%d" % n, align_bytes=64)
            raw = k_raw[c][:, h * ZONES : (h + 1) * ZONES]
            nc.vector.tensor_copy(
                out=k_words[c, h][:].rearrange("p t (a m y) -> p a t m y", m=8, y=2),
                in_=raw.rearrange("p (a m t y) -> p a t m y", m=8, t=SLOTS, y=2),
            )

        def sort_kern_scales(stack, passes):
            if passes.start == 0:
                ks_sorted[stack] = keep.tile([P, ZONES], U8, name="ks_sorted_%d" % stack, align_bytes=64)
                k_scales[STACK * stack] = ks_sorted[stack]
            nc.vector.tensor_copy(
                out=ks_sorted[stack][:].rearrange("p (h t m) -> p h t m", h=PASSES, t=SLOTS)[:, passes],
                in_=ks_raw[stack][:].rearrange("p (h m t) -> p h t m", h=PASSES, t=SLOTS)[:, passes],
            )

        def shift_kern_scales(c):
            stack, level = divmod(c, STACK)
            for q in range(QUADRANTS):
                at = 32 * q + 4 * level
                nc.sync.dma_start(
                    out=k_scales[c][32 * q : 32 * q + 4, :].bitcast(I32),
                    in_=ks_sorted[stack][at : at + 4, :].bitcast(I32),
                )

        def transpose_x(s, tiles, tag="x_bank"):
            n = tiles.stop - tiles.start
            bank = psum.tile([P, n, 2, P], F32, name=tag, tag=tag, bufs=2)
            for b in range(n):
                words = x_rows[s][:, tiles.start + b, :].bitcast(F32)
                for u in range(2):
                    nc.tensor.transpose(bank[:, b, u, :], words[:, u : STATIONS // 2 : 2], ident[:])
            x_bank[s, tiles.start] = bank

        def copy_x(s, tiles):
            n = tiles.stop - tiles.start
            group = work.tile([P, n, P, 2], F32, name="x_group", tag="x_group", bufs=3, align_bytes=64)
            nc.scalar.copy(out=group[:], in_=x_bank[s, tiles.start][:].rearrange("p b u n -> p b n u"))
            x_group[s, tiles.start] = group

        def quantize_x(s, tiles):
            n = tiles.stop - tiles.start
            codes = work.tile([P, n * P], U32, name="x_codes", tag="x_codes", bufs=5, align_bytes=64)
            scales = work.tile([P, n * P], U8, name="x_scales", tag="x_scales", bufs=5, align_bytes=64)
            nc.vector.quantize_mx(
                out=codes[:].bitcast(FP8X4),
                scales=scales[:],
                in_=x_group[s, tiles.start][:].rearrange("p b n u -> p (b n u)").bitcast(BF16),
            )
            for b in range(n):
                plans = slice(b * P, (b + 1) * P)
                x_codes[s, tiles.start + b], x_scales[s, tiles.start + b] = codes[:, plans], scales[:, plans]

        def first_matmul(s, h, b):
            c = s // 2
            bank = psum.tile([P, SLOTS, P], F32, name="logbusy", tag="logbusy", bufs=4)
            for t in range(SLOTS):
                at = (SLOTS * h + t) * P
                nc.tensor.matmul_mx(
                    out=bank[:, t, :],
                    lhsT=k_words[c, h][:, t, :].bitcast(FP4X4),
                    lhsT_scale=k_scales[c][:, at : at + P],
                    rhs=x_codes[s, b].bitcast(FP8X4),
                    rhs_scale=x_scales[s, b],
                    start=True,
                    stop=True,
                )
            logbusy[s, h, b] = bank

        def exponential(s, h, b):
            if b == 0:
                busy[s, h] = work.tile([P, 2, P, SLOTS], F32, name="busy", tag="busy", bufs=4)
            nc.scalar.activation(
                out=busy[s, h][:, b], in_=logbusy[s, h, b][:].rearrange("p t n -> p n t"), func=ACT.Exp
            )

        def cover(s, h, tiles):
            plans = (tiles.stop - tiles.start) * P
            if h == 0:
                covered[s, tiles.start] = work.tile(
                    [P, PASSES, plans, SLOTS], BF16, name="covered", tag="covered", bufs=3, align_bytes=64
                )
            row = PASSES * (s // 2) + h
            nc.vector.scalar_tensor_tensor(
                out=covered[s, tiles.start][:, h],
                in0=busy[s, h][:, tiles].rearrange("p b n t -> p (b n) t"),
                scalar=1.0,
                in1=d_neg[:, row : row + 1, :].to_broadcast([P, plans, SLOTS]),
                op0=ALU.subtract,
                op1=ALU.mult,
            )

        def quantize_covered(s, tiles, passes):
            plans = (tiles.stop - tiles.start) * P
            n = passes.stop - passes.start
            codes = work.tile([P, n, plans], U32, name="c_codes", tag="c_codes", bufs=4, align_bytes=64)
            scales = work.tile([P, n, plans], U8, name="c_scales", tag="c_scales", bufs=4, align_bytes=64)
            nc.vector.quantize_mx(
                out=codes[:].rearrange("p h n -> p (h n)").bitcast(FP8X4),
                scales=scales[:].rearrange("p h n -> p (h n)"),
                in_=covered[s, tiles.start][:, passes].rearrange("p h n t -> p (h n t)"),
            )
            for b in range(tiles.start, tiles.stop):
                cols = slice((b - tiles.start) * P, (b - tiles.start + 1) * P)
                for h in range(n):
                    c_codes[s, b, passes.start + h] = codes[:, h, cols]
                    c_scales[s, b, passes.start + h] = scales[:, h, cols]

        def second_pass(bank, s, b, h, readouts):
            c = s // 2
            nc.tensor.matmul_mx(
                out=bank[:],
                lhsT=c_codes[s, b, h].bitcast(FP8X4),
                lhsT_scale=c_scales[s, b, h],
                rhs=r_words[c][:, h, 2 * readouts.start : 2 * readouts.stop].bitcast(FP4X4),
                rhs_scale=r_scales[:, PASSES * c + h, readouts],
                start=(h == 0),
                stop=(h == PASSES - 1),
            )

        def second_matmul(s, b, tag="sums"):
            sums[s, b] = psum.tile([P, READOUTS], F32, name=tag, tag=tag, bufs=2)
            for h in range(PASSES):
                second_pass(sums[s, b], s, b, h, slice(0, READOUTS))

        def store(s, b, copy=nc.scalar.copy):
            if b == 0:
                result[s] = work.tile([P, 2, READOUTS], F32, name="result", tag="result", bufs=3)
            copy(out=result[s][:, b, :], in_=sums[s, b][:])
            nc.sync.dma_start(out=plan_rows(out, s)[:, b : b + 1, :], in_=result[s][:, b : b + 1, :])

        nc.vector.memset(ks_raw[0][:].bitcast(I32), 0)
        nc.vector.memset(ks_raw[1][:].bitcast(I32), 0)
        for c in shifted:
            nc.vector.memset(k_scales[c][:].bitcast(I32), 0)
        make_identity(nc, ident[:])
        nc.gpsimd.memset(r_scales[:].bitcast(I32), 0)

        load_x(0)
        load_kern(0)
        load_kern_scales(0)
        load_x(1)
        load_kern(1)
        nc.sync.dma_start(out=d_raw[:], in_=demand.rearrange("c (h p t) -> p (c h) t", h=PASSES, t=SLOTS))
        load_kern(2)
        load_x(2)
        load_x(3)
        load_read_scales(0)
        load_read(0)
        load_x(4)

        for tile in (FIRST, SECOND):
            transpose_x(0, tile)
            copy_x(0, tile)
        sort_kern_words(0)
        sort_kern_scales(0, FIRST)
        quantize_x(0, FIRST)
        quantize_x(0, SECOND)
        sort_kern_scales(0, SECOND)
        sort_kern_words(1)
        transpose_x(1, BOTH, "sums")
        copy_x(1, BOTH)
        sort_kern_words(2)
        quantize_x(1, BOTH)
        nc.vector.tensor_scalar(out=d_neg[:], in0=d_raw[:], scalar1=-1.0, scalar2=None, op0=ALU.mult)
        for n in range(3, SORT_AHEAD):
            sort_kern_words(n)
        shift_kern_scales(1)

        last = STEPS - 1
        for s in range(last):
            c, half = divmod(s, 2)
            turn, behind = s + TURN_AHEAD, s - OUT_BEHIND

            if half == 0 and c + 3 < PERIODS:
                load_kern(c + 3)
            if s + LOAD_AHEAD < STEPS:
                load_x(s + LOAD_AHEAD)
            if half == 0 and c + 1 < PERIODS:
                load_read(c + 1)
            if half == 1 and c % 2 == 0 and c + 2 < PERIODS:
                load_read_scales(c + 2)
            if s == 0:
                load_kern_scales(1)
            if half == 1 and c + 2 in shifted:
                shift_kern_scales(c + 2)

            first_matmul(s, 0, 0)
            first_matmul(s, 0, 1)
            exponential(s, 0, 0)
            exponential(s, 0, 1)
            first_matmul(s, 1, 0)
            if behind >= 0:
                second_matmul(behind, 0)
                store(behind, 0, nc.vector.tensor_copy if s >= VECTOR_OUT_FROM else nc.scalar.copy)
            first_matmul(s, 1, 1)
            if behind >= 0:
                second_matmul(behind, 1)
            if turn < STEPS:
                transpose_x(turn, BOTH)
            exponential(s, 1, 0)
            exponential(s, 1, 1)
            if turn < STEPS:
                copy_x(turn, BOTH)
            if behind >= 0:
                store(behind, 1)

            cover(s, 0, BOTH)
            if s >= 1:
                quantize_covered(s - 1, BOTH, BOTH)
            cover(s, 1, BOTH)
            if behind < 0:
                quantize_x(turn, BOTH)
            if s + SORT_AHEAD < PERIODS * PASSES:
                sort_kern_words(s + SORT_AHEAD)
            if s == STACK - 1:
                sort_kern_scales(1, BOTH)
            if behind >= 0 and turn < STEPS:
                quantize_x(turn, BOTH)

        behind, before = last - OUT_BEHIND, last - 1
        first_matmul(last, 0, 0)
        first_matmul(last, 1, 0)
        exponential(last, 0, 0)
        exponential(last, 1, 0)
        second_matmul(behind, 0)
        store(behind, 0)
        first_matmul(last, 0, 1)
        first_matmul(last, 1, 1)
        second_matmul(behind, 1)
        exponential(last, 0, 1)
        exponential(last, 1, 1)
        store(behind, 1)
        cover(last, 0, FIRST)
        quantize_covered(before, BOTH, BOTH)
        second_matmul(before, 0, "x_bank")
        second_matmul(before, 1, "x_bank")
        cover(last, 1, FIRST)
        cover(last, 0, SECOND)
        quantize_covered(last, FIRST, BOTH)
        quantize_covered(last, SECOND, FIRST)
        store(before, 0)
        store(before, 1)
        second_matmul(last, 0)

        columns = [slice(q * P, (q + 1) * P) for q in range(READOUTS // P)]
        quarters = [psum.tile([P, P], F32, name="logbusy", tag="logbusy", bufs=4) for cols in columns]
        for bank, cols in zip(quarters, columns):
            second_pass(bank, last, 1, 0, cols)
        cover(last, 1, SECOND)
        quantize_covered(last, SECOND, SECOND)
        for bank, cols in zip(quarters, columns):
            second_pass(bank, last, 1, 1, cols)
        store(last, 0)
        for pair, copy in enumerate((nc.vector.tensor_copy, nc.scalar.copy)):
            for q in (2 * pair, 2 * pair + 1):
                copy(out=result[last][:, 1, columns[q]], in_=quarters[q][:])
            both_columns = slice(2 * pair * P, 2 * (pair + 1) * P)
            nc.sync.dma_start(out=plan_rows(out, last)[:, 1, both_columns], in_=result[last][:, 1, both_columns])
